import numpy as np
import ml_dtypes


def mxq(x, axis, fmt="e4m3"):
    dtype, down = {"e4m3": (ml_dtypes.float8_e4m3fn, 7), "e5m2": (ml_dtypes.float8_e5m2, 14)}[fmt]
    v = np.moveaxis(np.asarray(x, np.float32).astype(ml_dtypes.bfloat16).astype(np.float64), axis, -1)
    blocks = v.reshape(v.shape[:-1] + (-1, 32))
    amax = np.abs(blocks).max(-1, keepdims=True)
    byte = np.maximum(np.where(amax > 0, np.frexp(amax)[1] - 1 + 127, 0) - down, 1)
    scale = np.exp2(byte - 127.0)
    codes = (blocks / scale).astype(np.float32).astype(dtype).astype(np.float64)
    return np.moveaxis((codes * scale).reshape(v.shape), -1, axis)


WIDE = False


def mx_kscale(k):
    if not WIDE:
        return np.ones(k)
    levels = np.array([10, -10, 5, -5, 0])
    if k % 512:
        return np.exp2(np.random.permutation(np.resize(levels, k // 32))).repeat(32)
    a = np.empty((k // 512, 16))
    for p in range(k // 512):
        a[p, :8] = np.random.permutation(np.resize(levels, 8))
        for g in range(8):
            far = levels[np.abs(levels - a[p, g]) >= 10]
            a[p, g + 8] = far[np.random.randint(len(far))]
    return np.exp2(a.ravel()).repeat(32)


def f64(x):
    return np.asarray(x).astype(np.float64)


def striped(idx):
    return np.tile(np.asarray(idx).reshape(-1, 16).T, (8, 1)).astype(np.uint16)


def unstriped(offs):
    return offs[:16].T.reshape(-1).astype(np.int64)


E2M1 = np.array([0.0, 0.5, 1.0, 1.5, 2.0, 3.0, 4.0, 6.0, -0.0, -0.5, -1.0, -1.5, -2.0, -3.0, -4.0, -6.0])


def pack_weight(w, fmt):
    k, n = w.shape
    w = f64(np.asarray(w, np.float32).astype(ml_dtypes.bfloat16)).reshape(k // 32, 32, n)
    amax = np.abs(w).max(1)
    if fmt == "e4m3":
        byte = np.frexp(amax)[1] - 1 + 127 - 7
    else:
        mant, ex = np.frexp(amax / 6.0)
        byte = np.where(mant > 0.5, ex, ex - 1) + 127
    byte = np.clip(np.where(amax > 0, byte, 1), 1, 254)
    scaled = (w * np.exp2(127.0 - byte)[:, None, :]).reshape(k, n).astype(np.float32)
    by_word = np.ascontiguousarray(scaled.reshape(k // 512, 128, 4, n).transpose(0, 1, 3, 2))
    if fmt == "e4m3":
        words = by_word.astype(ml_dtypes.float8_e4m3fn).view(np.uint8)
    else:
        c = by_word.astype(ml_dtypes.float4_e2m1fn).view(np.uint8) & 0xF
        words = (c[..., 0::2] | (c[..., 1::2] << 4)).reshape(k // 512, 128, 2 * n)
    return np.ascontiguousarray(words), np.ascontiguousarray(byte.astype(np.uint8).reshape(k // 512, 16, n))


def unpack_weight(words, scales, fmt):
    g, _, n = scales.shape
    words = np.ascontiguousarray(words).reshape(g, 128, n, -1)
    if fmt == "e4m3":
        vals = words.view(ml_dtypes.float8_e4m3fn).astype(np.float64)
    else:
        nib = np.empty((g, 128, n, 4), np.uint8)
        nib[..., 0::2] = words & 0xF
        nib[..., 1::2] = words >> 4
        vals = E2M1[nib]
    vals = vals * np.repeat(np.exp2(scales.astype(np.float64) - 127.0), 8, axis=1)[..., None]
    return vals.transpose(0, 1, 3, 2).reshape(g * 512, n)


def bf(x):
    return np.asarray(x, np.float32).astype(ml_dtypes.bfloat16)


def planes(Y):
    r, m = Y.shape
    b = f64(bf(Y)).reshape(r // 32, 32, m)
    amax = np.abs(b).max(1)
    byte = np.clip(np.where(amax > 0, np.frexp(amax)[1] - 1 + 127 - 7, 1), 1, 254)
    codes = (b * np.exp2(127.0 - byte)[:, None, :]).reshape(r, m).astype(np.float32).astype(ml_dtypes.float8_e4m3fn).view(np.uint8)
    words = codes.reshape(r // 512, 128, 4, m).transpose(0, 1, 3, 2)
    return np.ascontiguousarray(words), np.ascontiguousarray(byte.astype(np.uint8).reshape(r // 512, 16, m))


D, T, I, Q, E, J, M = 512, 2048, 512, 256, 512, 512, 512


def setup_inputs():
    n = np.random.standard_normal
    idx = np.random.permutation(T)[:I]
    fd = mx_kscale(D)
    fj = mx_kscale(J)
    fi = mx_kscale(I)
    fm = mx_kscale(M)
    ti = np.ones(T)
    ti[idx] = fi
    keysp = pack_weight(n((D, T)) / fd[:, None], "e2m1")
    return {
        "query": (n((D, Q)) * 0.4 / np.sqrt(D) * fd[:, None]).astype(np.float32),
        "ckey": (n((D, J)) / fd[:, None]).astype(np.float32),
        "cval": (n((J, E)) / fj[:, None]).astype(np.float32),
        "keys_words": keysp[0],
        "keys_scales": keysp[1],
        "vals": (n((E, T)) / ti).astype(np.float32),
        "wkey": (n((D, M)) / fd[:, None]).astype(np.float32),
        "wval": (n((M, E)) / fm[:, None]).astype(np.float32),
        "gc": (np.random.uniform(0.2, 1.0, (Q, 1))).astype(np.float32),
        "gs": (np.random.uniform(0.2, 1.0, (Q, 1))).astype(np.float32),
        "gw": (np.random.uniform(0.2, 1.0, (Q, 1))).astype(np.float32),
        "cf": (np.random.uniform(0.5, 2.0, (1, J)) * fj).astype(np.float32),
        "size": (np.random.uniform(0.5, 2.0, (1, I)) * fi).astype(np.float32),
        "mf": (np.random.uniform(0.5, 2.0, (1, M)) * fm).astype(np.float32),
        "offs": striped(idx),
    }


def reference(query, ckey, cval, keys_words, keys_scales, vals, wkey, wval, gc, gs, gw, cf, size, mf, offs):
    idx = unstriped(offs)
    keysu = unpack_weight(keys_words, keys_scales, "e2m1")
    queryq = mxq(f64(query), 0, "e4m3")
    ckeyq = mxq(f64(ckey), 0, "e4m3")
    a = queryq.T @ ckeyq
    keysidxg = keysu[:, idx]
    b = queryq.T @ keysidxg
    wkeyq = mxq(f64(wkey), 0, "e4m3")
    s = queryq.T @ wkeyq
    pc = np.exp(a - np.max(a, axis=1, keepdims=True))
    wc = pc * f64(gc) * f64(cf) / np.sum(pc, axis=1, keepdims=True)
    wtc = wc.T
    ps = np.exp(b - np.max(b, axis=1, keepdims=True))
    ws = ps * f64(gs) * f64(size) / np.sum(ps, axis=1, keepdims=True)
    wts = ws.T
    pw = np.exp(s - np.max(s, axis=1, keepdims=True))
    ww = pw * f64(gw) * f64(mf) / np.sum(pw, axis=1, keepdims=True)
    wtw = ww.T
    vt = f64(vals)[:, idx].T
    cvalq = mxq(f64(cval), 0, "e4m3")
    wtcq = mxq(wtc, 0, "e4m3")
    vtq = mxq(vt, 0, "e4m3")
    wtsq = mxq(wts, 0, "e4m3")
    wvalq = mxq(f64(wval), 0, "e4m3")
    wtwq = mxq(wtw, 0, "e4m3")
    o = cvalq.T @ wtcq + vtq.T @ wtsq + wvalq.T @ wtwq
    words, scales = planes(o)
    return o, words, scales

@@ -1,0 +1,255 @@
+from contextlib import ExitStack
+
+import concourse.mybir as mybir
+from concourse.masks import make_identity
+
+D, T, SLOTS, Q, E = 512, 2048, 512, 256, 512
+FLOPS = 2 * 3 * Q * D * SLOTS + 2 * 3 * E * SLOTS * Q
+
+F32 = mybir.dt.float32
+BF16 = mybir.dt.bfloat16
+I32 = mybir.dt.int32
+U32 = mybir.dt.uint32
+U16 = mybir.dt.uint16
+U8 = mybir.dt.uint8
+FP8X4 = mybir.dt.float8_e4m3fn_x4
+FP4X4 = mybir.dt.float4_e2m1fn_x4
+ALU = mybir.AluOpType
+ACT = mybir.ActivationFunctionType
+AXIS = mybir.AxisListType
+
+P = 128
+PACK = 4
+QBLOCKS = Q // P
+
+
+def tile_attend_nsa_branches_pl_kernel(tc, query, ckey, cval, keys_words, keys_scales, vals, wkey, wval,
+                                        gc, gs, gw, cf, size, mf, offs, out_0, out_1, out_2):
+    nc = tc.nc
+    with ExitStack() as ctx:
+        sb = ctx.enter_context(tc.tile_pool(name="sb", bufs=1))
+        ps = ctx.enter_context(tc.psum_pool(name="ps", bufs=1))
+
+        def held(name, shape, dtype, after=None):
+            return sb.tile(shape, dtype, name=name, tag=after or name, align_bytes=64)
+
+        def bank(b, name, shape):
+            return ps.tile(shape, F32, name=name, tag="bank%d" % b)
+
+        def load_rows(name, rows):
+            raw = held(name, [P, PACK, rows.shape[1]], F32)
+            nc.sync.dma_start(out=raw[:], in_=rows.rearrange("(p j) w -> p j w", j=PACK))
+            return raw
+
+        def copy_on(engine, out, in_):
+            if engine is nc.vector:
+                nc.vector.tensor_copy(out=out, in_=in_)
+            else:
+                nc.scalar.copy(out=out, in_=in_)
+
+        def weave(name, raw, vector_cols, dealt=False, scalar_pieces=1, after=None):
+            width = raw.shape[2]
+            woven = held(name, [P, width * PACK], BF16, after)
+            src = raw[:].rearrange("p j (c i) -> p c j i", i=PACK)
+            if dealt:
+                dst = woven[:].rearrange("p (i c j) -> p c j i", i=PACK, j=PACK)
+            else:
+                dst = woven[:].rearrange("p (c i j) -> p c j i", i=PACK, j=PACK)
+            cut = vector_cols // PACK
+            groups = width // PACK
+            if cut > 0:
+                nc.vector.tensor_copy(out=dst[:, :cut], in_=src[:, :cut])
+            piece = (groups - cut) // scalar_pieces
+            for c in range(cut, groups, piece):
+                nc.scalar.copy(out=dst[:, c:c + piece], in_=src[:, c:c + piece])
+            return woven
+
+        def quantize(name, woven, calls=1):
+            width = woven.shape[1] // PACK
+            codes = held(name + "_codes", [P, width], U32)
+            scales = held(name + "_scales", [P, width], U8)
+            step = width // calls
+            for c in range(0, width, step):
+                nc.vector.quantize_mx(out=codes[:, c:c + step].bitcast(FP8X4), scales=scales[:, c:c + step],
+                                      in_=woven[:, PACK * c:PACK * (c + step)])
+            return codes, scales
+
+        scale_pool = held("scale_pool", [P, T], U8)
+        nc.vector.memset(scale_pool[:].bitcast(I32), 0)
+        identity = held("identity", [P, P], F32)
+        make_identity(nc, identity[:])
+        token_weight = {}
+        gate = {}
+        for name, row in (("s", size), ("c", cf), ("w", mf)):
+            token_weight[name] = held("token_weight_" + name, [P, PACK], F32)
+            nc.sync.dma_start(out=token_weight[name][:], in_=row.rearrange("o (p t) -> (o p) t", t=PACK))
+        key_pool = held("key_pool", [P, T], U16)
+        nc.sync.dma_start(out=key_pool[:].bitcast(I32), in_=keys_words[0].bitcast(I32))
+        offsets = sb.tile([P, SLOTS // 16], U16, name="offsets")
+        nc.sync.dma_start(offsets[:], offs)
+        query_raw = load_rows("query_raw", query)
+        for quad in range(4):
+            nc.sync.dma_start(out=scale_pool[32 * quad:32 * quad + 4, :].bitcast(I32),
+                              in_=keys_scales[0, 4 * quad:4 * quad + 4, :].bitcast(I32))
+
+        def load_gate(name, column):
+            gate[name] = held("gate_" + name, [P, QBLOCKS], F32)
+            with nc.allow_non_contiguous_dma(reason="one gate a query row"):
+                nc.sync.dma_start(out=gate[name][:], in_=column.rearrange("(b p) o -> p (b o)", p=P))
+
+        vals_dealt = vals.rearrange("(p t) n -> p t n", t=PACK)
+        val_pool = {}
+
+        def load_vals(t):
+            pool_t = held("val_pool%d" % t, [P, T], F32)
+            nc.sync.dma_start(out=pool_t[:], in_=vals_dealt[:, t, :])
+            val_pool[t] = pool_t
+
+        ckey_raw = load_rows("ckey_raw", ckey)
+        load_gate("s", gs)
+        wkey_raw = load_rows("wkey_raw", wkey)
+        load_gate("c", gc)
+        load_gate("w", gw)
+        load_vals(0)
+        load_vals(1)
+        cval_raw = load_rows("cval_raw", cval)
+        load_vals(2)
+        load_vals(3)
+        wval_raw = load_rows("wval_raw", wval)
+
+        def scores(name, banks, q, keys, key_scales):
+            tiles = []
+            for b in range(QBLOCKS):
+                s = bank(banks[b], "score_%s%d" % (name, b), [P, SLOTS])
+                cols = slice(b * P, (b + 1) * P)
+                nc.tensor.matmul_mx(out=s[:], lhsT=q[0][:, cols].bitcast(FP8X4), lhsT_scale=q[1][:, cols],
+                                    rhs=keys, rhs_scale=key_scales, start=True, stop=True)
+                tiles.append(s)
+            return tiles
+
+        def spread(name, b):
+            wide = bank(b, "spread_" + name, [P, PACK, P])
+            for t in range(PACK):
+                nc.tensor.transpose(wide[:, t, :], token_weight[name][:, t:t + 1].to_broadcast([P, P]), identity[:])
+            return wide
+
+        neg_max = {name: held("neg_max_" + name, [P, QBLOCKS], F32) for name in "scw"}
+        total = {name: held("total_" + name, [P, QBLOCKS], F32) for name in "scw"}
+
+        def exponentials(name, score_tiles):
+            probs = []
+            for b in range(QBLOCKS):
+                nc.vector.tensor_reduce(out=neg_max[name][:, b:b + 1], in_=score_tiles[b][:], axis=AXIS.X, op=ALU.max,
+                                        negate=True)
+                p = held("prob_%s%d" % (name, b), [P, SLOTS], F32)
+                nc.scalar.activation(out=p[:], in_=score_tiles[b][:], func=ACT.Exp, bias=neg_max[name][:, b:b + 1],
+                                     scale=1.0, accum_out=total[name][:, b:b + 1])
+                probs.append(p)
+            return probs
+
+        def row_factor(name):
+            inverse = held("inverse_" + name, [P, QBLOCKS], F32)
+            factor = held("factor_" + name, [P, QBLOCKS], F32)
+            nc.vector.reciprocal(out=inverse[:], in_=total[name][:])
+            nc.vector.tensor_tensor(out=factor[:], in0=inverse[:], in1=gate[name][:], op=ALU.mult)
+            return factor
+
+        def weights(name, probs, factor, wide, b_turn):
+            turned = bank(b_turn, "turned_" + name, [P, 2, Q])
+            for b in range(QBLOCKS):
+                w = held("weight_%s%d" % (name, b), [P, SLOTS], BF16)
+                nc.vector.scalar_tensor_tensor(
+                    out=w[:].rearrange("q (p t) -> q p t", t=PACK), in0=probs[b][:].rearrange("q (p t) -> q p t", t=PACK),
+                    scalar=factor[:, b:b + 1], in1=wide[:].rearrange("q t p -> q p t"), op0=ALU.mult, op1=ALU.mult)
+                pairs = w[:].bitcast(F32)
+                for u in range(2):
+                    nc.tensor.transpose(turned[:, u, b * P:(b + 1) * P], pairs[:, u::2], identity[:])
+            woven = held("weight_woven_" + name, [P, Q * PACK], BF16)
+            nc.scalar.copy(out=woven[:].bitcast(F32).rearrange("p (q u) -> p q u", u=2),
+                           in_=turned[:].rearrange("p u q -> p q u"))
+            return woven
+
+        def gather_vals(t, b_turn, after, on_scalar):
+            picked = held("val_picked%d" % t, [P, SLOTS], BF16, None if on_scalar else after)
+            if on_scalar:
+                rounded = held("val_rounded%d" % t, [P, T], BF16, after)
+                for c in range(0, T, SLOTS):
+                    nc.scalar.copy(out=rounded[:, c:c + SLOTS], in_=val_pool[t][:, c:c + SLOTS])
+                nc.scalar.activation(out=picked[:], in_=rounded[:].indirect(offsets[:]), func=ACT.Copy)
+            else:
+                nc.vector.tensor_copy(out=picked[:], in_=val_pool[t][:].indirect(offsets[:]))
+            pairs = picked[:].bitcast(F32)
+            turned = bank(b_turn, "val_turned%d" % t, [P, 2, P])
+            for u in range(2):
+                nc.tensor.transpose(turned[:, u, :], pairs[:, u::2], identity[:])
+            woven = held("val_woven%d" % t, [P, P * PACK], BF16)
+            nc.scalar.copy(out=woven[:].bitcast(F32).rearrange("p (e u) -> p e u", u=2),
+                           in_=turned[:].rearrange("p u e -> p e u"))
+            return woven
+
+        def product(t, values, cols, w):
+            passes[t] = passes[t] + 1
+            nc.tensor.matmul_mx(out=acc[t][:], lhsT=values[0][:, cols].bitcast(FP8X4), lhsT_scale=values[1][:, cols],
+                                rhs=w[0][:].bitcast(FP8X4), rhs_scale=w[1][:], start=passes[t] == 1, stop=passes[t] == 3)
+            if passes[t] == 3:
+                copy_on(nc.scalar if t % 2 == 0 else nc.vector, result[:, t, :], acc[t][:])
+                if t % 2 == 1:
+                    nc.sync.dma_start(out=out_rows[:, t - 1:t + 1, :], in_=result[:, t - 1:t + 1, :])
+
+        whole = slice(0, P)
+        v_woven = {}
+        passes = [0] * PACK
+        result = held("result", [P, PACK, Q], F32)
+        out_rows = out_0.rearrange("(p t) q -> p t q", t=PACK)
+        key_picked = held("key_picked", [P, SLOTS], U16)
+        nc.vector.tensor_copy(out=key_picked[:], in_=key_pool[:].indirect(offsets[:]))
+        query_woven = weave("query_woven", query_raw, 0)
+        scale_picked = held("scale_picked", [P, SLOTS], U8)
+        nc.vector.tensor_copy(out=scale_picked[:], in_=scale_pool[:].indirect(offsets[:]))
+        q = quantize("query", query_woven)
+        score_s = scores("s", (3, 4), q, key_picked[:].bitcast(FP4X4), scale_picked[:])
+        wide_s = spread("s", 0)
+        wide_c = spread("c", 1)
+        wide_w = spread("w", 2)
+        ckey_woven = weave("ckey_woven", ckey_raw, 256, scalar_pieces=1, after=None)
+        ck = quantize("ckey", ckey_woven)
+        score_c = scores("c", (5, 6), q, ck[0][:].bitcast(FP8X4), ck[1][:])
+        wkey_woven = weave("wkey_woven", wkey_raw, 256, scalar_pieces=2, after=None)
+        wk = quantize("wkey", wkey_woven)
+        score_w = scores("w", (3, 4), q, wk[0][:].bitcast(FP8X4), wk[1][:])
+        probs_s = exponentials("s", score_s)
+        probs_c = exponentials("c", score_c)
+        probs_w = exponentials("w", score_w)
+        factor_s = row_factor("s")
+        factor_c = row_factor("c")
+        factor_w = row_factor("w")
+        ws_woven = weights("s", probs_s, factor_s, wide_s, 7)
+        wc_woven = weights("c", probs_c, factor_c, wide_c, 0)
+        ww_woven = weights("w", probs_w, factor_w, wide_w, 1)
+        acc = [bank(b, "acc%d" % t, [P, Q]) for t, b in enumerate((5, 6, 3, 4))]
+        ws = quantize("ws", ws_woven)
+        wc = quantize("wc", wc_woven)
+        ww = quantize("ww", ww_woven)
+        v_woven[0] = gather_vals(0, 7, "neg_max_s", False)
+        v_woven[1] = gather_vals(1, 0, "prob_s1", False)
+        v_woven[2] = gather_vals(2, 7, "prob_c1", False)
+        v_woven[3] = gather_vals(3, 2, "prob_w1", False)
+        product(0, quantize("v0", v_woven[0]), whole, ws)
+        product(1, quantize("v1", v_woven[1]), whole, ws)
+        cval_woven = weave("cval_woven", cval_raw, 0, dealt=True, scalar_pieces=4, after="neg_max_w")
+        cv = quantize("cval", cval_woven, calls=1)
+        for t in range(PACK):
+            product(t, cv, slice(t * P, (t + 1) * P), wc)
+        product(2, quantize("v2", v_woven[2]), whole, ws)
+        product(3, quantize("v3", v_woven[3]), whole, ws)
+        wval_woven = weave("wval_woven", wval_raw, 192, dealt=True, scalar_pieces=1, after="val_pool3")
+        wv = quantize("wval", wval_woven, calls=4)
+        for t in range(PACK):
+            product(t, wv, slice(t * P, (t + 1) * P), ww)
+        result_woven = weave("result_woven", result, 176)
+        codes, scales = quantize("result", result_woven)
+        nc.sync.dma_start(out=out_1[0].rearrange("p c r -> p (c r)").bitcast(I32), in_=codes[:].bitcast(I32))
+        for quad in range(4):
+            queue = nc.scalar if quad % 2 == 0 else nc.sync
+            queue.dma_start(out=out_2[0, 4 * quad:4 * quad + 4, :].bitcast(I32),
+                            in_=scales[32 * quad:32 * quad + 4, :].bitcast(I32))

@@ -47,26 +47,15 @@ def tile_attend_nsa_branches_pl_kernel(tc, query, ckey, cval, keys_words, keys_s
             else:
                 nc.scalar.copy(out=out, in_=in_)
 
-        def weave(name, raw, vector_cols, dealt=False, scalar_pieces=1, after=None):
-            width = raw.shape[2]
-            woven = held(name, [P, width * PACK], BF16, after)
-            src = raw[:].rearrange("p j (c i) -> p c j i", i=PACK)
-            if dealt:
-                dst = woven[:].rearrange("p (i c j) -> p c j i", i=PACK, j=PACK)
-            else:
-                dst = woven[:].rearrange("p (c i j) -> p c j i", i=PACK, j=PACK)
-            cut = vector_cols // PACK
-            groups = width // PACK
-            if cut > 0:
-                nc.vector.tensor_copy(out=dst[:, :cut], in_=src[:, :cut])
-            piece = (groups - cut) // scalar_pieces
-            for c in range(cut, groups, piece):
-                nc.scalar.copy(out=dst[:, c:c + piece], in_=src[:, c:c + piece])
-            return woven
+        def weave(engine, woven, raw, first, dealt=False):
+            groups = raw.shape[2] // PACK
+            pattern = "p (i c j) -> p c j i" if dealt else "p (c i j) -> p c j i"
+            dst = woven[:].rearrange(pattern, i=PACK, j=PACK)
+            copy_on(engine, dst[:, first // PACK:first // PACK + groups], raw.rearrange("p j (c i) -> p c j i", i=PACK))
 
-        def quantize(name, woven, calls=1):
+        def quantize(name, woven, calls=1, after=None, into=None):
             width = woven.shape[1] // PACK
-            codes = held(name + "_codes", [P, width], U32)
+            codes = held(name + "_codes", [P, width], U32, after) if into is None else into
             scales = held(name + "_scales", [P, width], U8)
             step = width // calls
             for c in range(0, width, step):
@@ -80,9 +69,22 @@ def tile_attend_nsa_branches_pl_kernel(tc, query, ckey, cval, keys_words, keys_s
         make_identity(nc, identity[:])
         token_weight = {}
         gate = {}
-        for name, row in (("s", size), ("c", cf), ("w", mf)):
+        val_pool = {}
+        vals_dealt = vals.rearrange("(p t) n -> p t n", t=PACK)
+
+        def load_token_weight(name, row):
             token_weight[name] = held("token_weight_" + name, [P, PACK], F32)
             nc.sync.dma_start(out=token_weight[name][:], in_=row.rearrange("o (p t) -> (o p) t", t=PACK))
+
+        def load_gate(name, column):
+            gate[name] = held("gate_" + name, [P, QBLOCKS], F32)
+            with nc.allow_non_contiguous_dma(reason="one gate a query row"):
+                nc.sync.dma_start(out=gate[name][:], in_=column.rearrange("(b p) o -> p (b o)", p=P))
+
+        def load_vals(t):
+            val_pool[t] = held("val_pool%d" % t, [P, T], F32)
+            nc.sync.dma_start(out=val_pool[t][:], in_=vals_dealt[:, t, :])
+
         key_pool = held("key_pool", [P, T], U16)
         nc.sync.dma_start(out=key_pool[:].bitcast(I32), in_=keys_words[0].bitcast(I32))
         offsets = sb.tile([P, SLOTS // 16], U16, name="offsets")
@@ -91,31 +93,21 @@ def tile_attend_nsa_branches_pl_kernel(tc, query, ckey, cval, keys_words, keys_s
         for quad in range(4):
             nc.sync.dma_start(out=scale_pool[32 * quad:32 * quad + 4, :].bitcast(I32),
                               in_=keys_scales[0, 4 * quad:4 * quad + 4, :].bitcast(I32))
-
-        def load_gate(name, column):
-            gate[name] = held("gate_" + name, [P, QBLOCKS], F32)
-            with nc.allow_non_contiguous_dma(reason="one gate a query row"):
-                nc.sync.dma_start(out=gate[name][:], in_=column.rearrange("(b p) o -> p (b o)", p=P))
-
-        vals_dealt = vals.rearrange("(p t) n -> p t n", t=PACK)
-        val_pool = {}
-
-        def load_vals(t):
-            pool_t = held("val_pool%d" % t, [P, T], F32)
-            nc.sync.dma_start(out=pool_t[:], in_=vals_dealt[:, t, :])
-            val_pool[t] = pool_t
-
-        ckey_raw = load_rows("ckey_raw", ckey)
+        ckey_a = load_rows("ckey_a", ckey[:, :256])
+        ckey_b = load_rows("ckey_b", ckey[:, 256:])
+        load_token_weight("s", size)
         load_gate("s", gs)
         wkey_raw = load_rows("wkey_raw", wkey)
+        load_token_weight("c", cf)
+        load_token_weight("w", mf)
+        load_vals(0)
         load_gate("c", gc)
         load_gate("w", gw)
-        load_vals(0)
-        load_vals(1)
         cval_raw = load_rows("cval_raw", cval)
+        load_vals(1)
+        wval_raw = load_rows("wval_raw", wval)
         load_vals(2)
         load_vals(3)
-        wval_raw = load_rows("wval_raw", wval)
 
         def scores(name, banks, q, keys, key_scales):
             tiles = []
@@ -133,22 +125,20 @@ def tile_attend_nsa_branches_pl_kernel(tc, query, ckey, cval, keys_words, keys_s
                 nc.tensor.transpose(wide[:, t, :], token_weight[name][:, t:t + 1].to_broadcast([P, P]), identity[:])
             return wide
 
-        neg_max = {name: held("neg_max_" + name, [P, QBLOCKS], F32) for name in "scw"}
         total = {name: held("total_" + name, [P, QBLOCKS], F32) for name in "scw"}
 
-        def exponentials(name, score_tiles):
-            probs = []
+        def exponentials(name, score_tiles, after=None, max_after=None):
+            probs = held("prob_" + name, [P, QBLOCKS, SLOTS], F32, after)
             for b in range(QBLOCKS):
-                nc.vector.tensor_reduce(out=neg_max[name][:, b:b + 1], in_=score_tiles[b][:], axis=AXIS.X, op=ALU.max,
+                neg_max = held("neg_max_%s%d" % (name, b), [P, 1], F32, max_after[b])
+                nc.vector.tensor_reduce(out=neg_max[:], in_=score_tiles[b][:], axis=AXIS.X, op=ALU.max,
                                         negate=True)
-                p = held("prob_%s%d" % (name, b), [P, SLOTS], F32)
-                nc.scalar.activation(out=p[:], in_=score_tiles[b][:], func=ACT.Exp, bias=neg_max[name][:, b:b + 1],
+                nc.scalar.activation(out=probs[:, b, :], in_=score_tiles[b][:], func=ACT.Exp, bias=neg_max[:],
                                      scale=1.0, accum_out=total[name][:, b:b + 1])
-                probs.append(p)
             return probs
 
-        def row_factor(name):
-            inverse = held("inverse_" + name, [P, QBLOCKS], F32)
+        def row_factor(name, after=None):
+            inverse = held("inverse_" + name, [P, QBLOCKS], F32, after)
             factor = held("factor_" + name, [P, QBLOCKS], F32)
             nc.vector.reciprocal(out=inverse[:], in_=total[name][:])
             nc.vector.tensor_tensor(out=factor[:], in0=inverse[:], in1=gate[name][:], op=ALU.mult)
@@ -159,94 +149,105 @@ def tile_attend_nsa_branches_pl_kernel(tc, query, ckey, cval, keys_words, keys_s
             for b in range(QBLOCKS):
                 w = held("weight_%s%d" % (name, b), [P, SLOTS], BF16)
                 nc.vector.scalar_tensor_tensor(
-                    out=w[:].rearrange("q (p t) -> q p t", t=PACK), in0=probs[b][:].rearrange("q (p t) -> q p t", t=PACK),
+                    out=w[:].rearrange("q (p t) -> q p t", t=PACK), in0=probs[:, b, :].rearrange("q (p t) -> q p t", t=PACK),
                     scalar=factor[:, b:b + 1], in1=wide[:].rearrange("q t p -> q p t"), op0=ALU.mult, op1=ALU.mult)
                 pairs = w[:].bitcast(F32)
                 for u in range(2):
                     nc.tensor.transpose(turned[:, u, b * P:(b + 1) * P], pairs[:, u::2], identity[:])
-            woven = held("weight_woven_" + name, [P, Q * PACK], BF16)
-            nc.scalar.copy(out=woven[:].bitcast(F32).rearrange("p (q u) -> p q u", u=2),
-                           in_=turned[:].rearrange("p u q -> p q u"))
-            return woven
+            return turned
 
-        def gather_vals(t, b_turn, after, on_scalar):
-            picked = held("val_picked%d" % t, [P, SLOTS], BF16, None if on_scalar else after)
-            if on_scalar:
-                rounded = held("val_rounded%d" % t, [P, T], BF16, after)
-                for c in range(0, T, SLOTS):
-                    nc.scalar.copy(out=rounded[:, c:c + SLOTS], in_=val_pool[t][:, c:c + SLOTS])
-                nc.scalar.activation(out=picked[:], in_=rounded[:].indirect(offsets[:]), func=ACT.Copy)
-            else:
-                nc.vector.tensor_copy(out=picked[:], in_=val_pool[t][:].indirect(offsets[:]))
+        def gather_vals(t, turned, place, after=None):
+            picked = held("val_picked%d" % t, [P, SLOTS], BF16, after)
+            nc.vector.tensor_copy(out=picked[:], in_=val_pool[t][:].indirect(offsets[:]))
             pairs = picked[:].bitcast(F32)
-            turned = bank(b_turn, "val_turned%d" % t, [P, 2, P])
             for u in range(2):
-                nc.tensor.transpose(turned[:, u, :], pairs[:, u::2], identity[:])
-            woven = held("val_woven%d" % t, [P, P * PACK], BF16)
+                nc.tensor.transpose(turned[:, u, place * P:(place + 1) * P], pairs[:, u::2], identity[:])
+
+        def weave_turned(name, turned, after=None):
+            woven = held(name, [P, turned.shape[2] * PACK], BF16, after)
             nc.scalar.copy(out=woven[:].bitcast(F32).rearrange("p (e u) -> p e u", u=2),
                            in_=turned[:].rearrange("p u e -> p e u"))
             return woven
 
-        def product(t, values, cols, w):
+        passes = [0] * PACK
+        result = held("result", [P, PACK, Q], F32)
+        out_rows = out_0.rearrange("(p t) q -> p t q", t=PACK)
+
+        def product(t, values, place, w):
+            cols = slice(place * P, (place + 1) * P)
             passes[t] = passes[t] + 1
             nc.tensor.matmul_mx(out=acc[t][:], lhsT=values[0][:, cols].bitcast(FP8X4), lhsT_scale=values[1][:, cols],
                                 rhs=w[0][:].bitcast(FP8X4), rhs_scale=w[1][:], start=passes[t] == 1, stop=passes[t] == 3)
             if passes[t] == 3:
-                copy_on(nc.scalar if t % 2 == 0 else nc.vector, result[:, t, :], acc[t][:])
+                copy_on(nc.scalar if t != 3 else nc.vector, result[:, t, :], acc[t][:])
                 if t % 2 == 1:
                     nc.sync.dma_start(out=out_rows[:, t - 1:t + 1, :], in_=result[:, t - 1:t + 1, :])
 
-        whole = slice(0, P)
-        v_woven = {}
-        passes = [0] * PACK
-        result = held("result", [P, PACK, Q], F32)
-        out_rows = out_0.rearrange("(p t) q -> p t q", t=PACK)
         key_picked = held("key_picked", [P, SLOTS], U16)
         nc.vector.tensor_copy(out=key_picked[:], in_=key_pool[:].indirect(offsets[:]))
-        query_woven = weave("query_woven", query_raw, 0)
+        query_woven = held("query_woven", [P, Q * PACK], BF16)
+        weave(nc.scalar, query_woven, query_raw[:], 0)
         scale_picked = held("scale_picked", [P, SLOTS], U8)
         nc.vector.tensor_copy(out=scale_picked[:], in_=scale_pool[:].indirect(offsets[:]))
-        q = quantize("query", query_woven)
-        score_s = scores("s", (3, 4), q, key_picked[:].bitcast(FP4X4), scale_picked[:])
-        wide_s = spread("s", 0)
-        wide_c = spread("c", 1)
-        wide_w = spread("w", 2)
-        ckey_woven = weave("ckey_woven", ckey_raw, 256, scalar_pieces=1, after=None)
-        ck = quantize("ckey", ckey_woven)
-        score_c = scores("c", (5, 6), q, ck[0][:].bitcast(FP8X4), ck[1][:])
-        wkey_woven = weave("wkey_woven", wkey_raw, 256, scalar_pieces=2, after=None)
-        wk = quantize("wkey", wkey_woven)
-        score_w = scores("w", (3, 4), q, wk[0][:].bitcast(FP8X4), wk[1][:])
-        probs_s = exponentials("s", score_s)
-        probs_c = exponentials("c", score_c)
-        probs_w = exponentials("w", score_w)
-        factor_s = row_factor("s")
+        q = quantize("query", query_woven, after="scale_pool")
+        score_s = scores("s", (3,4), q, key_picked[:].bitcast(FP4X4), scale_picked[:])
+        ckey_woven = held("ckey_woven", [P, SLOTS * PACK], BF16, None)
+        weave(nc.scalar, ckey_woven, ckey_a[:], 0)
+        weave(nc.vector, ckey_woven, ckey_b[:], 256)
+        ck = quantize("ckey", ckey_woven, after=None)
+        score_c = scores("c", (5,6), q, ck[0][:].bitcast(FP8X4), ck[1][:])
+        wkey_woven = held("wkey_woven", [P, SLOTS * PACK], BF16, None)
+        weave(nc.scalar, wkey_woven, wkey_raw[:], 0)
+        probs_s = exponentials("s", score_s, after="wkey_raw", max_after=("ckey_woven", "ckey_b"))
+        probs_c = exponentials("c", score_c, after="ckey_b", max_after=(None, None))
+        wide_s = spread("s", 7)
+        wide_c = spread("c", 0)
+        wide_w = spread("w", 1)
+        wk = quantize("wkey", wkey_woven, after=None)
+        score_w = scores("w", (3,4), q, wk[0][:].bitcast(FP8X4), wk[1][:])
+        turned_low = bank(2, "val_turned_low", [P, 2, 2 * P])
+        gather_vals(0, turned_low, 0, None)
+        cval_woven = held("cval_woven", [P, SLOTS * PACK], BF16, None)
+        weave(nc.scalar, cval_woven, cval_raw[:], 0, dealt=True)
+        probs_w = exponentials("w", score_w, after="cval_raw", max_after=("val_pool0", None))
+        factor_s = row_factor("s", after="val_picked0")
         factor_c = row_factor("c")
+        turned_s = weights("s", probs_s, factor_s, wide_s, 5)
+        turned_c = weights("c", probs_c, factor_c, wide_c, 6)
         factor_w = row_factor("w")
-        ws_woven = weights("s", probs_s, factor_s, wide_s, 7)
-        wc_woven = weights("c", probs_c, factor_c, wide_c, 0)
-        ww_woven = weights("w", probs_w, factor_w, wide_w, 1)
-        acc = [bank(b, "acc%d" % t, [P, Q]) for t, b in enumerate((5, 6, 3, 4))]
-        ws = quantize("ws", ws_woven)
-        wc = quantize("wc", wc_woven)
-        ww = quantize("ww", ww_woven)
-        v_woven[0] = gather_vals(0, 7, "neg_max_s", False)
-        v_woven[1] = gather_vals(1, 0, "prob_s1", False)
-        v_woven[2] = gather_vals(2, 7, "prob_c1", False)
-        v_woven[3] = gather_vals(3, 2, "prob_w1", False)
-        product(0, quantize("v0", v_woven[0]), whole, ws)
-        product(1, quantize("v1", v_woven[1]), whole, ws)
-        cval_woven = weave("cval_woven", cval_raw, 0, dealt=True, scalar_pieces=4, after="neg_max_w")
-        cv = quantize("cval", cval_woven, calls=1)
+        ws_woven = weave_turned("weight_woven_s", turned_s, "val_pool0")
+        wc_woven = weave_turned("weight_woven_c", turned_c, "neg_max_w1")
+        turned_w = weights("w", probs_w, factor_w, wide_w, 7)
+        wval_woven = held("wval_woven", [P, SLOTS * PACK], BF16, None)
+        weave(nc.scalar, wval_woven, wval_raw[:], 0, dealt=True)
+        gather_vals(1, turned_low, 1, None)
+        low_woven = weave_turned("val_woven_low", turned_low, "wval_raw")
+        ww_woven = weave_turned("weight_woven_w", turned_w, "val_pool2")
+        acc = [bank(b, "acc%d" % t, [P, Q]) for t, b in enumerate((5,6,3,4))]
+        turned2 = bank(0, "val_turned2", [P, 2, P])
+        gather_vals(2, turned2, 0, None)
+        woven2 = weave_turned("val_woven2", turned2, None)
+        ws = quantize("ws", ws_woven, after=None)
+        wc = quantize("wc", wc_woven, after=None)
+        cv = quantize("cval", cval_woven, after=None)
         for t in range(PACK):
-            product(t, cv, slice(t * P, (t + 1) * P), wc)
-        product(2, quantize("v2", v_woven[2]), whole, ws)
-        product(3, quantize("v3", v_woven[3]), whole, ws)
-        wval_woven = weave("wval_woven", wval_raw, 192, dealt=True, scalar_pieces=1, after="val_pool3")
-        wv = quantize("wval", wval_woven, calls=4)
+            product(t, cv, t, wc)
+        low = quantize("val_low", low_woven)
+        for t in range(2):
+            product(t, low, t, ws)
+        turned3 = bank(1, "val_turned3", [P, 2, P])
+        gather_vals(3, turned3, 0, None)
+        woven3 = weave_turned("val_woven3", turned3, None)
+        late = held("late_codes", [P, 768], U32, "val_pool3")
+        ww = quantize("ww", ww_woven, into=late[:, 0:256])
+        wv = quantize("wval", wval_woven, calls=4, into=late[:, 256:768])
         for t in range(PACK):
-            product(t, wv, slice(t * P, (t + 1) * P), ww)
-        result_woven = weave("result_woven", result, 176)
+            product(t, wv, t, ww)
+        product(2, quantize("val2", woven2, after="wval_woven"), 0, ws)
+        product(3, quantize("val3", woven3, after=None), 0, ws)
+        result_woven = held("result_woven", [P, Q * PACK], BF16)
+        weave(nc.vector, result_woven, result[:, :, :176], 0)
+        weave(nc.scalar, result_woven, result[:, :, 176:], 176)
         codes, scales = quantize("result", result_woven)
         nc.sync.dma_start(out=out_1[0].rearrange("p c r -> p (c r)").bitcast(I32), in_=codes[:].bitcast(I32))
         for quad in range(4):

from contextlib import ExitStack

import concourse.mybir as mybir
from concourse.masks import make_identity

D, T, SLOTS, Q, E = 512, 2048, 512, 256, 512
FLOPS = 2 * 3 * Q * D * SLOTS + 2 * 3 * E * SLOTS * Q

F32 = mybir.dt.float32
BF16 = mybir.dt.bfloat16
I32 = mybir.dt.int32
U32 = mybir.dt.uint32
U16 = mybir.dt.uint16
U8 = mybir.dt.uint8
FP8X4 = mybir.dt.float8_e4m3fn_x4
FP4X4 = mybir.dt.float4_e2m1fn_x4
ALU = mybir.AluOpType
ACT = mybir.ActivationFunctionType
AXIS = mybir.AxisListType

P = 128
PACK = 4
QBLOCKS = Q // P


def tile_attend_nsa_branches_pl_kernel(tc, query, ckey, cval, keys_words, keys_scales, vals, wkey, wval,
                                        gc, gs, gw, cf, size, mf, offs, out_0, out_1, out_2):
    nc = tc.nc
    with ExitStack() as ctx:
        sb = ctx.enter_context(tc.tile_pool(name="sb", bufs=1))
        ps = ctx.enter_context(tc.psum_pool(name="ps", bufs=1))

        def held(name, shape, dtype, after=None):
            return sb.tile(shape, dtype, name=name, tag=after or name, align_bytes=64)

        def bank(b, name, shape):
            return ps.tile(shape, F32, name=name, tag="bank%d" % b)

        def load_rows(name, rows):
            raw = held(name, [P, PACK, rows.shape[1]], F32)
            nc.sync.dma_start(out=raw[:], in_=rows.rearrange("(p j) w -> p j w", j=PACK))
            return raw

        def copy_on(engine, out, in_):
            if engine is nc.vector:
                nc.vector.tensor_copy(out=out, in_=in_)
            else:
                nc.scalar.copy(out=out, in_=in_)

        def weave(engine, woven, raw, first, dealt=False):
            groups = raw.shape[2] // PACK
            pattern = "p (i c j) -> p c j i" if dealt else "p (c i j) -> p c j i"
            dst = woven[:].rearrange(pattern, i=PACK, j=PACK)
            copy_on(engine, dst[:, first // PACK:first // PACK + groups], raw.rearrange("p j (c i) -> p c j i", i=PACK))

        def quantize(name, woven, calls=1, after=None, into=None):
            width = woven.shape[1] // PACK
            codes = held(name + "_codes", [P, width], U32, after) if into is None else into
            scales = held(name + "_scales", [P, width], U8)
            step = width // calls
            for c in range(0, width, step):
                nc.vector.quantize_mx(out=codes[:, c:c + step].bitcast(FP8X4), scales=scales[:, c:c + step],
                                      in_=woven[:, PACK * c:PACK * (c + step)])
            return codes, scales

        scale_pool = held("scale_pool", [P, T], U8)
        nc.vector.memset(scale_pool[:].bitcast(I32), 0)
        identity = held("identity", [P, P], F32)
        make_identity(nc, identity[:])
        token_weight = {}
        gate = {}
        val_pool = {}
        vals_dealt = vals.rearrange("(p t) n -> p t n", t=PACK)

        def load_token_weight(name, row):
            token_weight[name] = held("token_weight_" + name, [P, PACK], F32)
            nc.sync.dma_start(out=token_weight[name][:], in_=row.rearrange("o (p t) -> (o p) t", t=PACK))

        def load_gate(name, column):
            gate[name] = held("gate_" + name, [P, QBLOCKS], F32)
            with nc.allow_non_contiguous_dma(reason="one gate a query row"):
                nc.sync.dma_start(out=gate[name][:], in_=column.rearrange("(b p) o -> p (b o)", p=P))

        def load_vals(t):
            val_pool[t] = held("val_pool%d" % t, [P, T], F32)
            nc.sync.dma_start(out=val_pool[t][:], in_=vals_dealt[:, t, :])

        key_pool = held("key_pool", [P, T], U16)
        nc.sync.dma_start(out=key_pool[:].bitcast(I32), in_=keys_words[0].bitcast(I32))
        offsets = sb.tile([P, SLOTS // 16], U16, name="offsets")
        nc.sync.dma_start(offsets[:], offs)
        query_raw = load_rows("query_raw", query)
        for quad in range(4):
            nc.sync.dma_start(out=scale_pool[32 * quad:32 * quad + 4, :].bitcast(I32),
                              in_=keys_scales[0, 4 * quad:4 * quad + 4, :].bitcast(I32))
        ckey_a = load_rows("ckey_a", ckey[:, :256])
        ckey_b = load_rows("ckey_b", ckey[:, 256:])
        load_token_weight("s", size)
        load_gate("s", gs)
        wkey_raw = load_rows("wkey_raw", wkey)
        load_token_weight("c", cf)
        load_token_weight("w", mf)
        load_vals(0)
        load_gate("c", gc)
        load_gate("w", gw)
        cval_raw = load_rows("cval_raw", cval)
        load_vals(1)
        wval_raw = load_rows("wval_raw", wval)
        load_vals(2)
        load_vals(3)

        def scores(name, banks, q, keys, key_scales):
            tiles = []
            for b in range(QBLOCKS):
                s = bank(banks[b], "score_%s%d" % (name, b), [P, SLOTS])
                cols = slice(b * P, (b + 1) * P)
                nc.tensor.matmul_mx(out=s[:], lhsT=q[0][:, cols].bitcast(FP8X4), lhsT_scale=q[1][:, cols],
                                    rhs=keys, rhs_scale=key_scales, start=True, stop=True)
                tiles.append(s)
            return tiles

        def spread(name, b):
            wide = bank(b, "spread_" + name, [P, PACK, P])
            for t in range(PACK):
                nc.tensor.transpose(wide[:, t, :], token_weight[name][:, t:t + 1].to_broadcast([P, P]), identity[:])
            return wide

        total = {name: held("total_" + name, [P, QBLOCKS], F32) for name in "scw"}

        def exponentials(name, score_tiles, after=None, max_after=None):
            probs = held("prob_" + name, [P, QBLOCKS, SLOTS], F32, after)
            for b in range(QBLOCKS):
                neg_max = held("neg_max_%s%d" % (name, b), [P, 1], F32, max_after[b])
                nc.vector.tensor_reduce(out=neg_max[:], in_=score_tiles[b][:], axis=AXIS.X, op=ALU.max,
                                        negate=True)
                nc.scalar.activation(out=probs[:, b, :], in_=score_tiles[b][:], func=ACT.Exp, bias=neg_max[:],
                                     scale=1.0, accum_out=total[name][:, b:b + 1])
            return probs

        def row_factor(name, after=None):
            inverse = held("inverse_" + name, [P, QBLOCKS], F32, after)
            factor = held("factor_" + name, [P, QBLOCKS], F32)
            nc.vector.reciprocal(out=inverse[:], in_=total[name][:])
            nc.vector.tensor_tensor(out=factor[:], in0=inverse[:], in1=gate[name][:], op=ALU.mult)
            return factor

        def weights(name, probs, factor, wide, b_turn):
            turned = bank(b_turn, "turned_" + name, [P, 2, Q])
            for b in range(QBLOCKS):
                w = held("weight_%s%d" % (name, b), [P, SLOTS], BF16)
                nc.vector.scalar_tensor_tensor(
                    out=w[:].rearrange("q (p t) -> q p t", t=PACK), in0=probs[:, b, :].rearrange("q (p t) -> q p t", t=PACK),
                    scalar=factor[:, b:b + 1], in1=wide[:].rearrange("q t p -> q p t"), op0=ALU.mult, op1=ALU.mult)
                pairs = w[:].bitcast(F32)
                for u in range(2):
                    nc.tensor.transpose(turned[:, u, b * P:(b + 1) * P], pairs[:, u::2], identity[:])
            return turned

        def gather_vals(t, turned, place, after=None):
            picked = held("val_picked%d" % t, [P, SLOTS], BF16, after)
            nc.vector.tensor_copy(out=picked[:], in_=val_pool[t][:].indirect(offsets[:]))
            pairs = picked[:].bitcast(F32)
            for u in range(2):
                nc.tensor.transpose(turned[:, u, place * P:(place + 1) * P], pairs[:, u::2], identity[:])

        def weave_turned(name, turned, after=None):
            woven = held(name, [P, turned.shape[2] * PACK], BF16, after)
            nc.scalar.copy(out=woven[:].bitcast(F32).rearrange("p (e u) -> p e u", u=2),
                           in_=turned[:].rearrange("p u e -> p e u"))
            return woven

        passes = [0] * PACK
        result = held("result", [P, PACK, Q], F32)
        out_rows = out_0.rearrange("(p t) q -> p t q", t=PACK)

        def product(t, values, place, w):
            cols = slice(place * P, (place + 1) * P)
            passes[t] = passes[t] + 1
            nc.tensor.matmul_mx(out=acc[t][:], lhsT=values[0][:, cols].bitcast(FP8X4), lhsT_scale=values[1][:, cols],
                                rhs=w[0][:].bitcast(FP8X4), rhs_scale=w[1][:], start=passes[t] == 1, stop=passes[t] == 3)
            if passes[t] == 3:
                copy_on(nc.scalar if t != 3 else nc.vector, result[:, t, :], acc[t][:])
                if t % 2 == 1:
                    nc.sync.dma_start(out=out_rows[:, t - 1:t + 1, :], in_=result[:, t - 1:t + 1, :])

        key_picked = held("key_picked", [P, SLOTS], U16)
        nc.vector.tensor_copy(out=key_picked[:], in_=key_pool[:].indirect(offsets[:]))
        query_woven = held("query_woven", [P, Q * PACK], BF16)
        weave(nc.scalar, query_woven, query_raw[:], 0)
        scale_picked = held("scale_picked", [P, SLOTS], U8)
        nc.vector.tensor_copy(out=scale_picked[:], in_=scale_pool[:].indirect(offsets[:]))
        q = quantize("query", query_woven, after="scale_pool")
        score_s = scores("s", (3,4), q, key_picked[:].bitcast(FP4X4), scale_picked[:])
        ckey_woven = held("ckey_woven", [P, SLOTS * PACK], BF16, None)
        weave(nc.scalar, ckey_woven, ckey_a[:], 0)
        weave(nc.vector, ckey_woven, ckey_b[:], 256)
        ck = quantize("ckey", ckey_woven, after=None)
        score_c = scores("c", (5,6), q, ck[0][:].bitcast(FP8X4), ck[1][:])
        wkey_woven = held("wkey_woven", [P, SLOTS * PACK], BF16, None)
        weave(nc.scalar, wkey_woven, wkey_raw[:], 0)
        probs_s = exponentials("s", score_s, after="wkey_raw", max_after=("ckey_woven", "ckey_b"))
        probs_c = exponentials("c", score_c, after="ckey_b", max_after=(None, None))
        wide_s = spread("s", 7)
        wide_c = spread("c", 0)
        wide_w = spread("w", 1)
        wk = quantize("wkey", wkey_woven, after=None)
        score_w = scores("w", (3,4), q, wk[0][:].bitcast(FP8X4), wk[1][:])
        turned_low = bank(2, "val_turned_low", [P, 2, 2 * P])
        gather_vals(0, turned_low, 0, None)
        cval_woven = held("cval_woven", [P, SLOTS * PACK], BF16, None)
        weave(nc.scalar, cval_woven, cval_raw[:], 0, dealt=True)
        probs_w = exponentials("w", score_w, after="cval_raw", max_after=("val_pool0", None))
        factor_s = row_factor("s", after="val_picked0")
        factor_c = row_factor("c")
        turned_s = weights("s", probs_s, factor_s, wide_s, 5)
        turned_c = weights("c", probs_c, factor_c, wide_c, 6)
        factor_w = row_factor("w")
        ws_woven = weave_turned("weight_woven_s", turned_s, "val_pool0")
        wc_woven = weave_turned("weight_woven_c", turned_c, "neg_max_w1")
        turned_w = weights("w", probs_w, factor_w, wide_w, 7)
        wval_woven = held("wval_woven", [P, SLOTS * PACK], BF16, None)
        weave(nc.scalar, wval_woven, wval_raw[:], 0, dealt=True)
        gather_vals(1, turned_low, 1, None)
        low_woven = weave_turned("val_woven_low", turned_low, "wval_raw")
        ww_woven = weave_turned("weight_woven_w", turned_w, "val_pool2")
        acc = [bank(b, "acc%d" % t, [P, Q]) for t, b in enumerate((5,6,3,4))]
        turned2 = bank(0, "val_turned2", [P, 2, P])
        gather_vals(2, turned2, 0, None)
        woven2 = weave_turned("val_woven2", turned2, None)
        ws = quantize("ws", ws_woven, after=None)
        wc = quantize("wc", wc_woven, after=None)
        cv = quantize("cval", cval_woven, after=None)
        for t in range(PACK):
            product(t, cv, t, wc)
        low = quantize("val_low", low_woven)
        for t in range(2):
            product(t, low, t, ws)
        turned3 = bank(1, "val_turned3", [P, 2, P])
        gather_vals(3, turned3, 0, None)
        woven3 = weave_turned("val_woven3", turned3, None)
        late = held("late_codes", [P, 768], U32, "val_pool3")
        ww = quantize("ww", ww_woven, into=late[:, 0:256])
        wv = quantize("wval", wval_woven, calls=4, into=late[:, 256:768])
        for t in range(PACK):
            product(t, wv, t, ww)
        product(2, quantize("val2", woven2, after="wval_woven"), 0, ws)
        product(3, quantize("val3", woven3, after=None), 0, ws)
        result_woven = held("result_woven", [P, Q * PACK], BF16)
        weave(nc.vector, result_woven, result[:, :, :176], 0)
        weave(nc.scalar, result_woven, result[:, :, 176:], 176)
        codes, scales = quantize("result", result_woven)
        nc.sync.dma_start(out=out_1[0].rearrange("p c r -> p (c r)").bitcast(I32), in_=codes[:].bitcast(I32))
        for quad in range(4):
            queue = nc.scalar if quad % 2 == 0 else nc.sync
            queue.dma_start(out=out_2[0, 4 * quad:4 * quad + 4, :].bitcast(I32),
                            in_=scales[32 * quad:32 * quad + 4, :].bitcast(I32))
